import numpy as np
import ml_dtypes


def mxq(x, axis, fmt="e4m3"):
    dtype, down = {"e4m3": (ml_dtypes.float8_e4m3fn, 7), "e5m2": (ml_dtypes.float8_e5m2, 14)}[fmt]
    v = np.moveaxis(np.asarray(x, np.float32).astype(ml_dtypes.bfloat16).astype(np.float64), axis, -1)
    blocks = v.reshape(v.shape[:-1] + (-1, 32))
    amax = np.abs(blocks).max(-1, keepdims=True)
    byte = np.maximum(np.where(amax > 0, np.frexp(amax)[1] - 1 + 127, 0) - down, 1)
    scale = np.exp2(byte - 127.0)
    codes = (blocks / scale).astype(np.float32).astype(dtype).astype(np.float64)
    return np.moveaxis((codes * scale).reshape(v.shape), -1, axis)


WIDE = False


def mx_kscale(k):
    if not WIDE:
        return np.ones(k)
    levels = np.array([10, -10, 5, -5, 0])
    if k % 512:
        return np.exp2(np.random.permutation(np.resize(levels, k // 32))).repeat(32)
    a = np.empty((k // 512, 16))
    for p in range(k // 512):
        a[p, :8] = np.random.permutation(np.resize(levels, 8))
        for g in range(8):
            far = levels[np.abs(levels - a[p, g]) >= 10]
            a[p, g + 8] = far[np.random.randint(len(far))]
    return np.exp2(a.ravel()).repeat(32)


BF16 = ml_dtypes.bfloat16


def bf(x):
    return np.asarray(x, np.float32).astype(BF16)


def f64(x):
    return np.asarray(x).astype(np.float64)

E4M3FN = np.array([(-1.0 if i & 128 else 1.0) * ((1.0 + (i & 7) / 8.0) * 2.0 ** (((i >> 3) & 15) - 7) if i & 120 else (i & 7) * 2.0 ** -9) for i in range(256)])


def e4m3fn_bytes(y):
    return np.clip(np.asarray(y, np.float64), -448.0, 448.0).astype(np.float32).astype(ml_dtypes.float8_e4m3fn).view(np.uint8)


def e4m3fn_values(b):
    return E4M3FN[b]


T, K, N = 2048, 2048, 1024

FP8_MAX = 448.0


def setup_inputs():
    s = mx_kscale(K)
    size = 2.0 ** np.random.uniform(-1.0, 1.0, (T, 1))
    x = np.random.standard_normal((T, K)) * size * s
    x_scale = (np.abs(x).max(axis=1, keepdims=True) / FP8_MAX).astype(np.float32)
    w = 1.5 * np.random.standard_normal((N, K)) / np.sqrt(K) / s
    b = 0.5 * np.random.standard_normal(N)
    return {"x_bytes": e4m3fn_bytes(x / f64(x_scale)),
            "x_scale": x_scale,
            "w": bf(w),
            "b": bf(b)}


def reference(x_bytes, x_scale, w, b):
    x = e4m3fn_values(x_bytes) * np.repeat(f64(x_scale), K, axis=1)
    z = mxq(x, 1, "e4m3") @ mxq(f64(w), 1, "e4m3").T
    z = z + f64(b)
    return 1.0 / (1.0 + np.exp(-z))

@@ -1,0 +1,212 @@
+from contextlib import ExitStack
+
+import concourse.mybir as mybir
+from concourse.masks import make_identity
+
+T, K, N = 2048, 2048, 1024
+FLOPS = 2 * T * K * N
+
+F32 = mybir.dt.float32
+BF16 = mybir.dt.bfloat16
+U32 = mybir.dt.uint32
+U8 = mybir.dt.uint8
+FP8 = mybir.dt.float8_e4m3fn
+FP8X4 = mybir.dt.float8_e4m3fn_x4
+MULT = mybir.AluOpType.mult
+ADD = mybir.AluOpType.add
+SIGMOID = mybir.ActivationFunctionType.Sigmoid
+
+P = 128
+PASSES = 4
+X_TILES = T // P
+W_TILES = N // P
+HALF = 512
+
+LOADS = [('x', 0, 1), ('s', 0, 0), ('w', 0, 1), ('b', 0, 0), ('w', 1, 1), ('w', 2, 1), ('x', 1, 1), ('w', 3, 1), ('w', 4, 1), ('x', 2, 1), ('w', 5, 1), ('w', 6, 1), ('w', 7, 1), ('x', 3, 1), ('x', 4, 2), ('x', 6, 2), ('x', 8, 2), ('x', 10, 2), ('x', 12, 2), ('x', 14, 2)]
+ORDER = [
+    ('widen', 0), ('T', 'x', 0, 0), ('T', 'x', 0, 1), ('evac', 'x', 0, 0, 'S'), ('T', 'w', 0, 0), ('evac', 'x', 0, 1, 'V'),
+    ('T', 'w', 0, 1), ('bias',), ('evac', 'w', 0, 0, 'S'), ('quant', 'x', 0), ('T', 'w', 1, 0), ('evac', 'w', 0, 1, 'V'),
+    ('T', 'w', 1, 1), ('evac', 'w', 1, 0, 'S'), ('quant', 'w', 0), ('T', 'w', 2, 0), ('evac', 'w', 1, 1, 'S'), ('widen', 1),
+    ('T', 'w', 2, 1), ('evac', 'w', 2, 0, 'S'), ('evac', 'w', 2, 1, 'V'), ('T', 'x', 1, 0), ('T', 'x', 1, 1), ('evac', 'x', 1, 0, 'S'),
+    ('quant', 'w', 1), ('T', 'w', 3, 0), ('evac', 'x', 1, 1, 'S'), ('quant', 'w', 2), ('T', 'w', 3, 1), ('evac', 'w', 3, 0, 'S'),
+    ('widen', 2), ('T', 'w', 4, 0), ('evac', 'w', 3, 1, 'S'), ('T', 'w', 4, 1), ('evac', 'w', 4, 0, 'S'), ('quant', 'w', 3),
+    ('T', 'x', 2, 0), ('evac', 'w', 4, 1, 'S'), ('T', 'x', 2, 1), ('quant', 'x', 1), ('M', 0, 0), ('evac', 'x', 2, 0, 'S'),
+    ('quant', 'w', 4), ('evac', 'x', 2, 1, 'S'), ('T', 'w', 5, 0), ('add', 0, 0), ('T', 'w', 5, 1), ('widen', 3),
+    ('evac', 'w', 5, 0, 'S'), ('T', 'w', 6, 0), ('evac', 'w', 5, 1, 'S'), ('T', 'w', 6, 1), ('quant', 'x', 2), ('evac', 'w', 6, 0, 'S'),
+    ('M', 1, 0), ('quant', 'w', 5), ('evac', 'w', 6, 1, 'S'), ('sig', 0, 0), ('widen', 4), ('T', 'w', 7, 0),
+    ('T', 'w', 7, 1), ('add', 1, 0), ('evac', 'w', 7, 0, 'S'), ('T', 'x', 3, 0), ('quant', 'w', 6), ('evac', 'w', 7, 1, 'S'),
+    ('T', 'x', 3, 1), ('M', 2, 0), ('evac', 'x', 3, 0, 'S'), ('widen', 5), ('evac', 'x', 3, 1, 'S'), ('sig', 1, 0),
+    ('quant', 'w', 7), ('add', 2, 0), ('M', 0, 1), ('quant', 'x', 3), ('sig', 2, 0), ('widen', 6),
+    ('M', 1, 1), ('add', 0, 1), ('T', 'x', 4, 0), ('T', 'x', 4, 1), ('add', 1, 1), ('evac', 'x', 4, 0, 'S'),
+    ('T', 'x', 5, 0), ('widen', 7), ('evac', 'x', 4, 1, 'S'), ('T', 'x', 5, 1), ('M', 2, 1), ('sig', 0, 1),
+    ('evac', 'x', 5, 0, 'S'), ('quant', 'x', 4), ('M', 3, 0), ('evac', 'x', 5, 1, 'S'), ('add', 2, 1), ('sig', 1, 1),
+    ('widen', 8), ('M', 3, 1), ('sig', 2, 1), ('add', 3, 0), ('T', 'x', 6, 0), ('add', 3, 1),
+    ('sig', 3, 0), ('T', 'x', 6, 1), ('quant', 'x', 5), ('T', 'x', 7, 0), ('evac', 'x', 6, 1, 'S'), ('T', 'x', 7, 1),
+    ('widen', 9), ('evac', 'x', 6, 0, 'S'), ('M', 4, 0), ('evac', 'x', 7, 1, 'S'), ('quant', 'x', 6), ('evac', 'x', 7, 0, 'S'),
+    ('M', 4, 1), ('sig', 3, 1), ('add', 4, 0), ('quant', 'x', 7), ('sig', 4, 0), ('M', 5, 0),
+    ('add', 4, 1), ('widen', 10), ('M', 5, 1), ('sig', 4, 1), ('add', 5, 0), ('T', 'x', 8, 0),
+    ('T', 'x', 8, 1), ('add', 5, 1), ('evac', 'x', 8, 0, 'S'), ('T', 'x', 9, 0), ('widen', 11), ('evac', 'x', 8, 1, 'S'),
+    ('T', 'x', 9, 1), ('M', 6, 0), ('sig', 5, 0), ('evac', 'x', 9, 0, 'S'), ('quant', 'x', 8), ('M', 6, 1),
+    ('evac', 'x', 9, 1, 'S'), ('add', 6, 0), ('sig', 5, 1), ('widen', 12), ('M', 7, 0), ('sig', 6, 0),
+    ('add', 6, 1), ('M', 7, 1), ('add', 7, 0), ('sig', 6, 1), ('quant', 'x', 9), ('sig', 7, 0),
+    ('T', 'x', 10, 0), ('add', 7, 1), ('T', 'x', 10, 1), ('evac', 'x', 10, 0, 'S'), ('T', 'x', 11, 0), ('widen', 13),
+    ('evac', 'x', 10, 1, 'S'), ('T', 'x', 11, 1), ('M', 8, 0), ('evac', 'x', 11, 0, 'S'), ('quant', 'x', 10), ('evac', 'x', 11, 1, 'S'),
+    ('widen', 14), ('M', 8, 1), ('sig', 7, 1), ('add', 8, 0), ('M', 9, 0), ('add', 8, 1),
+    ('sig', 8, 0), ('quant', 'x', 11), ('M', 9, 1), ('sig', 8, 1), ('add', 9, 0), ('widen', 15),
+    ('T', 'x', 12, 0), ('sig', 9, 0), ('T', 'x', 12, 1), ('evac', 'x', 12, 0, 'S'), ('T', 'x', 13, 0), ('T', 'x', 13, 1),
+    ('add', 9, 1), ('evac', 'x', 12, 1, 'S'), ('M', 10, 0), ('evac', 'x', 13, 0, 'S'), ('quant', 'x', 12), ('evac', 'x', 13, 1, 'S'),
+    ('M', 10, 1), ('add', 10, 0), ('sig', 9, 1), ('quant', 'x', 13), ('sig', 10, 0), ('M', 11, 0),
+    ('add', 10, 1), ('sig', 10, 1), ('M', 11, 1), ('add', 11, 0), ('sig', 11, 0), ('T', 'x', 14, 0),
+    ('add', 11, 1), ('T', 'x', 14, 1), ('evac', 'x', 14, 0, 'S'), ('T', 'x', 15, 0), ('evac', 'x', 14, 1, 'S'), ('T', 'x', 15, 1),
+    ('M', 12, 0), ('evac', 'x', 15, 0, 'S'), ('quant', 'x', 14), ('evac', 'x', 15, 1, 'S'), ('M', 12, 1), ('sig', 11, 1),
+    ('add', 12, 0), ('quant', 'x', 15), ('sig', 12, 0), ('M', 13, 0), ('add', 12, 1), ('sig', 12, 1),
+    ('M', 13, 1), ('add', 13, 0), ('sig', 13, 0), ('M', 14, 0), ('add', 13, 1), ('sig', 13, 1),
+    ('M', 14, 1), ('add', 14, 0), ('sig', 14, 0), ('M', 15, 0), ('add', 14, 1), ('sig', 14, 1),
+    ('M', 15, 1), ('add', 15, 0), ('sig', 15, 0), ('add', 15, 1), ('sig', 15, 1),
+]
+WARM = 0
+
+
+def tile_fp8_activation_linear_probe_d3_kernel(tc, x_bytes, x_scale, w, b, out):
+    nc = tc.nc
+    x_rows = x_bytes.rearrange("(p i) k -> p i k", i=X_TILES)
+    out_rows = out.rearrange("(p i) n -> p i n", i=X_TILES)
+    w_rows = w.rearrange("(j p) k -> p j k", p=P)
+
+    with ExitStack() as ctx:
+        keep = ctx.enter_context(tc.tile_pool(name="keep", bufs=1))
+        wide_pool = ctx.enter_context(tc.tile_pool(name="wide", bufs=5))
+        grouped_pool = ctx.enter_context(tc.tile_pool(name="grouped", bufs=5))
+        result_pool = ctx.enter_context(tc.tile_pool(name="result", bufs=16))
+        turn_psum = ctx.enter_context(tc.psum_pool(name="turn", bufs=4))
+        acc_psum = ctx.enter_context(tc.psum_pool(name="acc", bufs=4))
+        ctx.enter_context(tc.manual_schedule())
+
+        xb = keep.tile([P, X_TILES, K], U8, name="xb", align_bytes=64)
+        wb = keep.tile([P, W_TILES, K], BF16, name="wb", align_bytes=64)
+        scale = keep.tile([P, X_TILES], F32, name="scale", align_bytes=64)
+        x_codes = keep.tile([P, X_TILES, PASSES, P], U32, name="x_codes", align_bytes=64)
+        x_scales = keep.tile([P, X_TILES, PASSES, P], U8, name="x_scales", align_bytes=64)
+        w_codes = keep.tile([P, PASSES, N], U32, name="w_codes", align_bytes=64)
+        w_scales = keep.tile([P, PASSES, N], U8, name="w_scales", align_bytes=64)
+        ident = keep.tile([P, P], F32, name="ident", align_bytes=64)
+        ones = keep.tile([P, P], BF16, name="ones", align_bytes=64)
+        b_row = keep.tile([P, N], BF16, name="b_row", align_bytes=64)
+        bias = keep.tile([P, N], BF16, name="bias", align_bytes=64)
+
+        make_identity(nc, ident[:])
+        nc.vector.memset(ones[:], 64.0)
+        nc.vector.memset(b_row[:], 0.0)
+        nc.scalar.activation(out=ones[:], in_=ones[:], func=SIGMOID)
+        if WARM:
+            junk = keep.tile([P, HALF], BF16, name="junk", align_bytes=64)
+            nc.vector.memset(junk[:], 1.0)
+            for r in range(WARM):
+                warm = acc_psum.tile([P, HALF], F32, name="acc", tag="acc")
+                nc.tensor.matmul(warm[:], lhsT=junk[:, 0:P], rhs=junk[:], start=True, stop=True)
+
+        for kind, first, count in LOADS:
+            if kind == "x":
+                nc.sync.dma_start(out=xb[:, first : first + count, :], in_=x_rows[:, first : first + count, :])
+            elif kind == "w":
+                nc.sync.dma_start(out=wb[:, first : first + count, :], in_=w_rows[:, first : first + count, :])
+            elif kind == "s":
+                nc.sync.dma_start(out=scale[:], in_=x_scale.rearrange("(p i) o -> p (i o)", i=X_TILES))
+            else:
+                nc.sync.dma_start(out=b_row[0:1, :], in_=b.rearrange("(o n) -> o n", o=1))
+
+        wide, banks, grouped, accs, results = {}, {}, {}, {}, {}
+
+        def spread_bias():
+            bank = acc_psum.tile([P, N], BF16, name="acc", tag="acc")
+            for h in range(2):
+                cols = slice(h * HALF, (h + 1) * HALF)
+                nc.tensor.matmul(bank[:, cols], lhsT=ones[:], rhs=b_row[:, cols], start=True, stop=True)
+            nc.scalar.copy(out=bias[:], in_=bank[:])
+
+        def widen(i):
+            t = wide_pool.tile([P, K], BF16, name="wide", tag="wide", align_bytes=64)
+            wide["x", i] = t
+            nc.vector.tensor_scalar(
+                out=t[:].rearrange("p (u c e) -> p c u e", u=2, e=2),
+                in0=xb[:, i, :].bitcast(FP8).rearrange("p (c u e) -> p c u e", u=2, e=2),
+                scalar1=scale[:, i : i + 1],
+                scalar2=None,
+                op0=MULT,
+            )
+
+        def unzip(j):
+            t = wide_pool.tile([P, K], BF16, name="wide", tag="wide", align_bytes=64)
+            wide["w", j] = t
+            nc.vector.tensor_copy(
+                out=t[:].bitcast(F32).rearrange("p (u c) -> p u c", u=2),
+                in_=wb[:, j, :].bitcast(F32).rearrange("p (c u) -> p u c", u=2),
+            )
+
+        def turn(kind, i, h):
+            bank = turn_psum.tile([P, 2, 2, P], F32, name="turn", tag="turn")
+            banks[kind, i, h] = bank
+            for gg in range(2):
+                g = 2 * h + gg
+                for u in range(2):
+                    if (kind, i) in wide:
+                        src = wide[kind, i][:].bitcast(F32)[:, 512 * u + P * g : 512 * u + P * (g + 1)]
+                    else:
+                        src = wb[:, i, :].bitcast(F32)[:, 256 * g + u : 256 * (g + 1) : 2]
+                    nc.tensor.transpose(bank[:, gg, u, :], src, ident[:])
+
+        def empty(kind, i, h, engine):
+            if (kind, i) not in grouped:
+                grouped[kind, i] = grouped_pool.tile([P, K], BF16, name="grouped", tag="grouped", align_bytes=64)
+            dst = grouped[kind, i][:, 1024 * h : 1024 * (h + 1)].bitcast(F32).rearrange("p (g r u) -> p g r u", g=2, u=2)
+            src = banks[kind, i, h][:].rearrange("p g u r -> p g r u")
+            if engine == "S":
+                nc.scalar.copy(out=dst, in_=src)
+            else:
+                nc.vector.tensor_copy(out=dst, in_=src)
+
+        def quantise(kind, i):
+            src = grouped[kind, i]
+            if kind == "x":
+                nc.vector.quantize_mx(
+                    out=x_codes[:, i, :, :].rearrange("p g r -> p (g r)").bitcast(FP8X4),
+                    scales=x_scales[:, i, :, :].rearrange("p g r -> p (g r)"),
+                    in_=src[:],
+                )
+            else:
+                for g in range(PASSES):
+                    nc.vector.quantize_mx(
+                        out=w_codes[:, g, P * i : P * (i + 1)].bitcast(FP8X4),
+                        scales=w_scales[:, g, P * i : P * (i + 1)],
+                        in_=src[:, 512 * g : 512 * (g + 1)],
+                    )
+
+        def multiply(i, h):
+            acc = acc_psum.tile([P, HALF], F32, name="acc", tag="acc")
+            accs[i, h] = acc
+            cols = slice(h * HALF, (h + 1) * HALF)
+            for g in range(PASSES):
+                nc.tensor.matmul_mx(
+                    out=acc[:],
+                    lhsT=x_codes[:, i, g, :].bitcast(FP8X4),
+                    lhsT_scale=x_scales[:, i, g, :],
+                    rhs=w_codes[:, g, cols].bitcast(FP8X4),
+                    rhs_scale=w_scales[:, g, cols],
+                    start=(g == 0),
+                    stop=(g == PASSES - 1),
+                )
+
+        def add_bias(i, h):
+            res = result_pool.tile([P, HALF], F32, name="res", tag="res", align_bytes=64)
+            results[i, h] = res
+            nc.vector.tensor_tensor(out=res[:], in0=accs[i, h][:], in1=bias[:, h * HALF : (h + 1) * HALF], op=ADD)
+
+        def finish(i, h):
+            res = results[i, h]
+            nc.scalar.activation(out=res[:], in_=res[:], func=SIGMOID)
+            nc.sync.dma_start(out=out_rows[:, i, h * HALF : (h + 1) * HALF], in_=res[:])
+
+        steps = {"bias": spread_bias, "widen": widen, "unz": unzip, "T": turn, "evac": empty, "quant": quantise,
+                 "M": multiply, "add": add_bias, "sig": finish}
+        for step in ORDER:
+            steps[step[0]](*step[1:])

@@ -14,6 +14,7 @@ FP8 = mybir.dt.float8_e4m3fn
 FP8X4 = mybir.dt.float8_e4m3fn_x4
 MULT = mybir.AluOpType.mult
 ADD = mybir.AluOpType.add
+COPY = mybir.ActivationFunctionType.Copy
 SIGMOID = mybir.ActivationFunctionType.Sigmoid
 
 P = 128
@@ -22,49 +23,50 @@ X_TILES = T // P
 W_TILES = N // P
 HALF = 512
 
-LOADS = [('x', 0, 1), ('s', 0, 0), ('w', 0, 1), ('b', 0, 0), ('w', 1, 1), ('w', 2, 1), ('x', 1, 1), ('w', 3, 1), ('w', 4, 1), ('x', 2, 1), ('w', 5, 1), ('w', 6, 1), ('w', 7, 1), ('x', 3, 1), ('x', 4, 2), ('x', 6, 2), ('x', 8, 2), ('x', 10, 2), ('x', 12, 2), ('x', 14, 2)]
+LOADS = [('w', 0, 1, 0), ('x', 0, 1, None), ('s', 0, 0, None), ('w', 0, 1, 1), ('b', 0, 0, None), ('w', 1, 1, None), ('w', 2, 1, None), ('x', 1, 1, None), ('w', 3, 1, None), ('x', 2, 1, None), ('w', 4, 1, None), ('w', 5, 1, None), ('w', 6, 1, None), ('x', 3, 1, None), ('w', 7, 1, None), ('x', 4, 2, None), ('x', 6, 2, None), ('x', 8, 2, None), ('x', 10, 2, None), ('x', 12, 2, None), ('x', 14, 2, None)]
 ORDER = [
-    ('widen', 0), ('T', 'x', 0, 0), ('T', 'x', 0, 1), ('evac', 'x', 0, 0, 'S'), ('T', 'w', 0, 0), ('evac', 'x', 0, 1, 'V'),
-    ('T', 'w', 0, 1), ('bias',), ('evac', 'w', 0, 0, 'S'), ('quant', 'x', 0), ('T', 'w', 1, 0), ('evac', 'w', 0, 1, 'V'),
-    ('T', 'w', 1, 1), ('evac', 'w', 1, 0, 'S'), ('quant', 'w', 0), ('T', 'w', 2, 0), ('evac', 'w', 1, 1, 'S'), ('widen', 1),
-    ('T', 'w', 2, 1), ('evac', 'w', 2, 0, 'S'), ('evac', 'w', 2, 1, 'V'), ('T', 'x', 1, 0), ('T', 'x', 1, 1), ('evac', 'x', 1, 0, 'S'),
-    ('quant', 'w', 1), ('T', 'w', 3, 0), ('evac', 'x', 1, 1, 'S'), ('quant', 'w', 2), ('T', 'w', 3, 1), ('evac', 'w', 3, 0, 'S'),
-    ('widen', 2), ('T', 'w', 4, 0), ('evac', 'w', 3, 1, 'S'), ('T', 'w', 4, 1), ('evac', 'w', 4, 0, 'S'), ('quant', 'w', 3),
-    ('T', 'x', 2, 0), ('evac', 'w', 4, 1, 'S'), ('T', 'x', 2, 1), ('quant', 'x', 1), ('M', 0, 0), ('evac', 'x', 2, 0, 'S'),
-    ('quant', 'w', 4), ('evac', 'x', 2, 1, 'S'), ('T', 'w', 5, 0), ('add', 0, 0), ('T', 'w', 5, 1), ('widen', 3),
-    ('evac', 'w', 5, 0, 'S'), ('T', 'w', 6, 0), ('evac', 'w', 5, 1, 'S'), ('T', 'w', 6, 1), ('quant', 'x', 2), ('evac', 'w', 6, 0, 'S'),
-    ('M', 1, 0), ('quant', 'w', 5), ('evac', 'w', 6, 1, 'S'), ('sig', 0, 0), ('widen', 4), ('T', 'w', 7, 0),
-    ('T', 'w', 7, 1), ('add', 1, 0), ('evac', 'w', 7, 0, 'S'), ('T', 'x', 3, 0), ('quant', 'w', 6), ('evac', 'w', 7, 1, 'S'),
-    ('T', 'x', 3, 1), ('M', 2, 0), ('evac', 'x', 3, 0, 'S'), ('widen', 5), ('evac', 'x', 3, 1, 'S'), ('sig', 1, 0),
-    ('quant', 'w', 7), ('add', 2, 0), ('M', 0, 1), ('quant', 'x', 3), ('sig', 2, 0), ('widen', 6),
-    ('M', 1, 1), ('add', 0, 1), ('T', 'x', 4, 0), ('T', 'x', 4, 1), ('add', 1, 1), ('evac', 'x', 4, 0, 'S'),
-    ('T', 'x', 5, 0), ('widen', 7), ('evac', 'x', 4, 1, 'S'), ('T', 'x', 5, 1), ('M', 2, 1), ('sig', 0, 1),
-    ('evac', 'x', 5, 0, 'S'), ('quant', 'x', 4), ('M', 3, 0), ('evac', 'x', 5, 1, 'S'), ('add', 2, 1), ('sig', 1, 1),
-    ('widen', 8), ('M', 3, 1), ('sig', 2, 1), ('add', 3, 0), ('T', 'x', 6, 0), ('add', 3, 1),
-    ('sig', 3, 0), ('T', 'x', 6, 1), ('quant', 'x', 5), ('T', 'x', 7, 0), ('evac', 'x', 6, 1, 'S'), ('T', 'x', 7, 1),
-    ('widen', 9), ('evac', 'x', 6, 0, 'S'), ('M', 4, 0), ('evac', 'x', 7, 1, 'S'), ('quant', 'x', 6), ('evac', 'x', 7, 0, 'S'),
-    ('M', 4, 1), ('sig', 3, 1), ('add', 4, 0), ('quant', 'x', 7), ('sig', 4, 0), ('M', 5, 0),
-    ('add', 4, 1), ('widen', 10), ('M', 5, 1), ('sig', 4, 1), ('add', 5, 0), ('T', 'x', 8, 0),
-    ('T', 'x', 8, 1), ('add', 5, 1), ('evac', 'x', 8, 0, 'S'), ('T', 'x', 9, 0), ('widen', 11), ('evac', 'x', 8, 1, 'S'),
-    ('T', 'x', 9, 1), ('M', 6, 0), ('sig', 5, 0), ('evac', 'x', 9, 0, 'S'), ('quant', 'x', 8), ('M', 6, 1),
-    ('evac', 'x', 9, 1, 'S'), ('add', 6, 0), ('sig', 5, 1), ('widen', 12), ('M', 7, 0), ('sig', 6, 0),
-    ('add', 6, 1), ('M', 7, 1), ('add', 7, 0), ('sig', 6, 1), ('quant', 'x', 9), ('sig', 7, 0),
-    ('T', 'x', 10, 0), ('add', 7, 1), ('T', 'x', 10, 1), ('evac', 'x', 10, 0, 'S'), ('T', 'x', 11, 0), ('widen', 13),
-    ('evac', 'x', 10, 1, 'S'), ('T', 'x', 11, 1), ('M', 8, 0), ('evac', 'x', 11, 0, 'S'), ('quant', 'x', 10), ('evac', 'x', 11, 1, 'S'),
-    ('widen', 14), ('M', 8, 1), ('sig', 7, 1), ('add', 8, 0), ('M', 9, 0), ('add', 8, 1),
-    ('sig', 8, 0), ('quant', 'x', 11), ('M', 9, 1), ('sig', 8, 1), ('add', 9, 0), ('widen', 15),
-    ('T', 'x', 12, 0), ('sig', 9, 0), ('T', 'x', 12, 1), ('evac', 'x', 12, 0, 'S'), ('T', 'x', 13, 0), ('T', 'x', 13, 1),
-    ('add', 9, 1), ('evac', 'x', 12, 1, 'S'), ('M', 10, 0), ('evac', 'x', 13, 0, 'S'), ('quant', 'x', 12), ('evac', 'x', 13, 1, 'S'),
-    ('M', 10, 1), ('add', 10, 0), ('sig', 9, 1), ('quant', 'x', 13), ('sig', 10, 0), ('M', 11, 0),
-    ('add', 10, 1), ('sig', 10, 1), ('M', 11, 1), ('add', 11, 0), ('sig', 11, 0), ('T', 'x', 14, 0),
-    ('add', 11, 1), ('T', 'x', 14, 1), ('evac', 'x', 14, 0, 'S'), ('T', 'x', 15, 0), ('evac', 'x', 14, 1, 'S'), ('T', 'x', 15, 1),
-    ('M', 12, 0), ('evac', 'x', 15, 0, 'S'), ('quant', 'x', 14), ('evac', 'x', 15, 1, 'S'), ('M', 12, 1), ('sig', 11, 1),
-    ('add', 12, 0), ('quant', 'x', 15), ('sig', 12, 0), ('M', 13, 0), ('add', 12, 1), ('sig', 12, 1),
-    ('M', 13, 1), ('add', 13, 0), ('sig', 13, 0), ('M', 14, 0), ('add', 13, 1), ('sig', 13, 1),
-    ('M', 14, 1), ('add', 14, 0), ('sig', 14, 0), ('M', 15, 0), ('add', 14, 1), ('sig', 14, 1),
-    ('M', 15, 1), ('add', 15, 0), ('sig', 15, 0), ('add', 15, 1), ('sig', 15, 1),
+    ('D', 6), ('widen', 0), ('T', 'w', 0, 0), ('T', 'w', 0, 1), ('evac', 'w', 0, 0, 'S'), ('evac', 'w', 0, 1, 'V'),
+    ('T', 'x', 0, 0), ('T', 'x', 0, 1), ('evac', 'x', 0, 0, 'S'), ('quant', 'w', 0), ('B',), ('evac', 'x', 0, 1, 'S'),
+    ('T', 'w', 1, 0), ('Bc',), ('quant', 'x', 0), ('T', 'w', 1, 1), ('evac', 'w', 1, 0, 'S'), ('D', 1),
+    ('widen', 1), ('T', 'w', 2, 0), ('evac', 'w', 1, 1, 'S'), ('T', 'w', 2, 1), ('evac', 'w', 2, 0, 'S'), ('quant', 'w', 1),
+    ('D', 1), ('evac', 'w', 2, 1, 'S'), ('T', 'x', 1, 0), ('widen', 2), ('T', 'x', 1, 1), ('evac', 'x', 1, 0, 'S'),
+    ('T', 'w', 3, 0), ('evac', 'x', 1, 1, 'S'), ('T', 'w', 3, 1), ('quant', 'w', 2), ('evac', 'w', 3, 0, 'S'), ('D', 1),
+    ('T', 'x', 2, 0), ('quant', 'x', 1), ('evac', 'w', 3, 1, 'S'), ('T', 'x', 2, 1), ('T', 'w', 4, 0), ('evac', 'x', 2, 0, 'S'),
+    ('quant', 'w', 3), ('T', 'w', 4, 1), ('evac', 'x', 2, 1, 'S'), ('M', 0, 0, 512), ('evac', 'w', 4, 0, 'S'), ('quant', 'x', 2),
+    ('evac', 'w', 4, 1, 'S'), ('widen', 3), ('M', 1, 0, 512), ('add', 0, 0, 512), ('T', 'w', 5, 0), ('add', 1, 0, 512),
+    ('sig', 0, 0, 512), ('T', 'w', 5, 1), ('widen', 4), ('evac', 'w', 5, 0, 'S'), ('T', 'w', 6, 0), ('evac', 'w', 5, 1, 'S'),
+    ('T', 'w', 6, 1), ('quant', 'w', 4), ('M', 2, 0, 512), ('evac', 'w', 6, 0, 'S'), ('evac', 'w', 6, 1, 'S'), ('quant', 'w', 5),
+    ('sig', 1, 0, 512), ('T', 'x', 3, 0), ('quant', 'w', 6), ('T', 'x', 3, 1), ('evac', 'x', 3, 0, 'S'), ('add', 2, 0, 512),
+    ('T', 'w', 7, 0), ('evac', 'x', 3, 1, 'S'), ('widen', 5), ('T', 'w', 7, 1), ('evac', 'w', 7, 0, 'S'), ('T', 'x', 4, 0),
+    ('T', 'x', 4, 1), ('evac', 'w', 7, 1, 'S'), ('quant', 'x', 3), ('sig', 2, 0, 512), ('quant', 'w', 7), ('M', 3, 0, 512),
+    ('evac', 'x', 4, 0, 'S'), ('widen', 6), ('evac', 'x', 4, 1, 'S'), ('M', 0, 512, 512), ('add', 3, 0, 512), ('quant', 'x', 4),
+    ('M', 1, 512, 512), ('sig', 3, 0, 512), ('add', 0, 512, 512), ('M', 2, 512, 512), ('add', 1, 512, 512), ('sig', 0, 512, 512),
+    ('widen', 7), ('sig', 1, 512, 512), ('T', 'x', 5, 0), ('T', 'x', 5, 1), ('evac', 'x', 5, 0, 'S'), ('add', 2, 512, 512),
+    ('T', 'x', 6, 0), ('T', 'x', 6, 1), ('evac', 'x', 5, 1, 'S'), ('widen', 8), ('M', 3, 512, 512), ('evac', 'x', 6, 0, 'S'),
+    ('evac', 'x', 6, 1, 'S'), ('quant', 'x', 5), ('M', 4, 0, 512), ('sig', 2, 512, 512), ('add', 3, 512, 512), ('quant', 'x', 6),
+    ('M', 4, 512, 512), ('sig', 3, 512, 512), ('add', 4, 0, 512), ('T', 'x', 7, 0), ('add', 4, 512, 512), ('sig', 4, 0, 512),
+    ('T', 'x', 7, 1), ('widen', 9), ('evac', 'x', 7, 0, 'S'), ('T', 'x', 8, 0), ('T', 'x', 8, 1), ('evac', 'x', 7, 1, 'S'),
+    ('M', 5, 0, 512), ('widen', 10), ('evac', 'x', 8, 0, 'S'), ('evac', 'x', 8, 1, 'S'), ('M', 5, 512, 512), ('sig', 4, 512, 512),
+    ('add', 5, 0, 512), ('quant', 'x', 7), ('sig', 5, 0, 512), ('M', 6, 0, 512), ('add', 5, 512, 512), ('quant', 'x', 8),
+    ('M', 6, 512, 512), ('sig', 5, 512, 512), ('add', 6, 0, 512), ('T', 'x', 9, 0), ('add', 6, 512, 512), ('sig', 6, 0, 512),
+    ('T', 'x', 9, 1), ('widen', 11), ('evac', 'x', 9, 0, 'S'), ('T', 'x', 10, 0), ('T', 'x', 10, 1), ('evac', 'x', 9, 1, 'S'),
+    ('M', 7, 0, 512), ('widen', 12), ('evac', 'x', 10, 0, 'S'), ('evac', 'x', 10, 1, 'S'), ('M', 7, 512, 512), ('sig', 6, 512, 512),
+    ('add', 7, 0, 512), ('quant', 'x', 9), ('sig', 7, 0, 512), ('M', 8, 0, 512), ('add', 7, 512, 512), ('quant', 'x', 10),
+    ('M', 8, 512, 512), ('sig', 7, 512, 512), ('add', 8, 0, 512), ('T', 'x', 11, 0), ('add', 8, 512, 512), ('sig', 8, 0, 512),
+    ('T', 'x', 11, 1), ('widen', 13), ('evac', 'x', 11, 0, 'S'), ('T', 'x', 12, 0), ('T', 'x', 12, 1), ('evac', 'x', 11, 1, 'S'),
+    ('M', 9, 0, 512), ('widen', 14), ('evac', 'x', 12, 0, 'S'), ('evac', 'x', 12, 1, 'S'), ('M', 9, 512, 512), ('sig', 8, 512, 512),
+    ('add', 9, 0, 512), ('quant', 'x', 11), ('sig', 9, 0, 512), ('M', 10, 0, 512), ('add', 9, 512, 512), ('quant', 'x', 12),
+    ('M', 10, 512, 512), ('sig', 9, 512, 512), ('add', 10, 0, 512), ('T', 'x', 13, 0), ('add', 10, 512, 512), ('sig', 10, 0, 512),
+    ('T', 'x', 13, 1), ('widen', 15), ('evac', 'x', 13, 0, 'S'), ('T', 'x', 14, 0), ('T', 'x', 14, 1), ('evac', 'x', 13, 1, 'S'),
+    ('M', 11, 0, 512), ('evac', 'x', 14, 0, 'S'), ('quant', 'x', 13), ('evac', 'x', 14, 1, 'S'), ('M', 11, 512, 512), ('add', 11, 0, 512),
+    ('sig', 10, 512, 512), ('quant', 'x', 14), ('sig', 11, 0, 512), ('M', 12, 0, 512), ('add', 11, 512, 512), ('sig', 11, 512, 512),
+    ('M', 12, 512, 512), ('add', 12, 0, 512), ('sig', 12, 0, 512), ('T', 'x', 15, 0), ('add', 12, 512, 512), ('T', 'x', 15, 1),
+    ('evac', 'x', 15, 0, 'S'), ('M', 13, 0, 512), ('evac', 'x', 15, 1, 'S'), ('sig', 12, 512, 512), ('quant', 'x', 15), ('M', 13, 512, 512),
+    ('add', 13, 0, 512), ('sig', 13, 0, 512), ('M', 14, 0, 512), ('add', 13, 512, 512), ('sig', 13, 512, 512), ('M', 14, 512, 512),
+    ('add', 14, 0, 512), ('sig', 14, 0, 512), ('M', 15, 0, 512), ('add', 14, 512, 512), ('sig', 14, 512, 512), ('M', 15, 512, 256),
+    ('add', 15, 0, 512), ('M', 15, 768, 256), ('add', 15, 512, 256), ('sig', 15, 0, 512), ('add', 15, 768, 256), ('sig', 15, 512, 256),
+    ('sig', 15, 768, 256),
 ]
-WARM = 0
 
 
 def tile_fp8_activation_linear_probe_d3_kernel(tc, x_bytes, x_scale, w, b, out):
@@ -94,35 +96,45 @@ def tile_fp8_activation_linear_probe_d3_kernel(tc, x_bytes, x_scale, w, b, out):
         b_row = keep.tile([P, N], BF16, name="b_row", align_bytes=64)
         bias = keep.tile([P, N], BF16, name="bias", align_bytes=64)
 
+        junk = keep.tile([P, HALF], BF16, name="junk", align_bytes=64)
         make_identity(nc, ident[:])
-        nc.vector.memset(ones[:], 64.0)
+        nc.vector.memset(junk[:], 1.0)
         nc.vector.memset(b_row[:], 0.0)
+        nc.vector.memset(ones[:], 64.0)
         nc.scalar.activation(out=ones[:], in_=ones[:], func=SIGMOID)
-        if WARM:
-            junk = keep.tile([P, HALF], BF16, name="junk", align_bytes=64)
-            nc.vector.memset(junk[:], 1.0)
-            for r in range(WARM):
-                warm = acc_psum.tile([P, HALF], F32, name="acc", tag="acc")
-                nc.tensor.matmul(warm[:], lhsT=junk[:, 0:P], rhs=junk[:], start=True, stop=True)
 
-        for kind, first, count in LOADS:
+        for kind, first, count, part in LOADS:
+            ks = slice(0, K) if part is None else slice(part * K // 2, (part + 1) * K // 2)
             if kind == "x":
-                nc.sync.dma_start(out=xb[:, first : first + count, :], in_=x_rows[:, first : first + count, :])
+                nc.sync.dma_start(out=xb[:, first : first + count, ks], in_=x_rows[:, first : first + count, ks])
             elif kind == "w":
-                nc.sync.dma_start(out=wb[:, first : first + count, :], in_=w_rows[:, first : first + count, :])
+                nc.sync.dma_start(out=wb[:, first : first + count, ks], in_=w_rows[:, first : first + count, ks])
             elif kind == "s":
                 nc.sync.dma_start(out=scale[:], in_=x_scale.rearrange("(p i) o -> p (i o)", i=X_TILES))
             else:
                 nc.sync.dma_start(out=b_row[0:1, :], in_=b.rearrange("(o n) -> o n", o=1))
 
-        wide, banks, grouped, accs, results = {}, {}, {}, {}, {}
+        wide, plain, banks, grouped, accs, results = {}, {}, {}, {}, {}, {}
 
         def spread_bias():
             bank = acc_psum.tile([P, N], BF16, name="acc", tag="acc")
+            banks["bias"] = bank
             for h in range(2):
                 cols = slice(h * HALF, (h + 1) * HALF)
                 nc.tensor.matmul(bank[:, cols], lhsT=ones[:], rhs=b_row[:, cols], start=True, stop=True)
-            nc.scalar.copy(out=bias[:], in_=bank[:])
+
+        def copy_bias():
+            nc.scalar.copy(out=bias[:], in_=banks["bias"][:])
+
+        def warm(count):
+            bank = acc_psum.tile([P, HALF], F32, name="acc", tag="acc")
+            for r in range(count):
+                nc.tensor.matmul(bank[:], lhsT=junk[:, 0:P], rhs=junk[:], start=True, stop=True)
+
+        def scalar_widen(i):
+            t = wide_pool.tile([P, K], BF16, name="wide", tag="wide", align_bytes=64)
+            plain["x", i] = t
+            nc.scalar.activation(out=t[:], in_=xb[:, i, :].bitcast(FP8), func=COPY, scale=scale[:, i : i + 1])
 
         def widen(i):
             t = wide_pool.tile([P, K], BF16, name="wide", tag="wide", align_bytes=64)
@@ -135,10 +147,10 @@ def tile_fp8_activation_linear_probe_d3_kernel(tc, x_bytes, x_scale, w, b, out):
                 op0=MULT,
             )
 
-        def unzip(j):
+        def unzip(j, engine):
             t = wide_pool.tile([P, K], BF16, name="wide", tag="wide", align_bytes=64)
             wide["w", j] = t
-            nc.vector.tensor_copy(
+            (nc.vector.tensor_copy if engine == "V" else nc.scalar.copy)(
                 out=t[:].bitcast(F32).rearrange("p (u c) -> p u c", u=2),
                 in_=wb[:, j, :].bitcast(F32).rearrange("p (c u) -> p u c", u=2),
             )
@@ -152,7 +164,8 @@ def tile_fp8_activation_linear_probe_d3_kernel(tc, x_bytes, x_scale, w, b, out):
                     if (kind, i) in wide:
                         src = wide[kind, i][:].bitcast(F32)[:, 512 * u + P * g : 512 * u + P * (g + 1)]
                     else:
-                        src = wb[:, i, :].bitcast(F32)[:, 256 * g + u : 256 * (g + 1) : 2]
+                        rows = plain[kind, i][:] if kind == "x" else wb[:, i, :]
+                        src = rows.bitcast(F32)[:, 256 * g + u : 256 * (g + 1) : 2]
                     nc.tensor.transpose(bank[:, gg, u, :], src, ident[:])
 
         def empty(kind, i, h, engine):
@@ -181,10 +194,10 @@ def tile_fp8_activation_linear_probe_d3_kernel(tc, x_bytes, x_scale, w, b, out):
                         in_=src[:, 512 * g : 512 * (g + 1)],
                     )
 
-        def multiply(i, h):
-            acc = acc_psum.tile([P, HALF], F32, name="acc", tag="acc")
-            accs[i, h] = acc
-            cols = slice(h * HALF, (h + 1) * HALF)
+        def multiply(i, c0, width):
+            acc = acc_psum.tile([P, width], F32, name="acc", tag="acc")
+            accs[i, c0] = acc
+            cols = slice(c0, c0 + width)
             for g in range(PASSES):
                 nc.tensor.matmul_mx(
                     out=acc[:],
@@ -196,17 +209,17 @@ def tile_fp8_activation_linear_probe_d3_kernel(tc, x_bytes, x_scale, w, b, out):
                     stop=(g == PASSES - 1),
                 )
 
-        def add_bias(i, h):
-            res = result_pool.tile([P, HALF], F32, name="res", tag="res", align_bytes=64)
-            results[i, h] = res
-            nc.vector.tensor_tensor(out=res[:], in0=accs[i, h][:], in1=bias[:, h * HALF : (h + 1) * HALF], op=ADD)
+        def add_bias(i, c0, width):
+            res = result_pool.tile([P, width], F32, name="res", tag="res", align_bytes=64)
+            results[i, c0] = res
+            nc.vector.tensor_tensor(out=res[:], in0=accs[i, c0][:], in1=bias[:, c0 : c0 + width], op=ADD)
 
-        def finish(i, h):
-            res = results[i, h]
+        def finish(i, c0, width):
+            res = results[i, c0]
             nc.scalar.activation(out=res[:], in_=res[:], func=SIGMOID)
-            nc.sync.dma_start(out=out_rows[:, i, h * HALF : (h + 1) * HALF], in_=res[:])
+            nc.sync.dma_start(out=out_rows[:, i, c0 : c0 + width], in_=res[:])
 
-        steps = {"bias": spread_bias, "widen": widen, "unz": unzip, "T": turn, "evac": empty, "quant": quantise,
-                 "M": multiply, "add": add_bias, "sig": finish}
+        steps = {"B": spread_bias, "Bc": copy_bias, "D": warm, "widen": widen, "swiden": scalar_widen, "unz": unzip, "T": turn,
+                 "evac": empty, "quant": quantise, "M": multiply, "add": add_bias, "sig": finish}
         for step in ORDER:
             steps[step[0]](*step[1:])

from contextlib import ExitStack

import concourse.mybir as mybir
from concourse.masks import make_identity

T, K, N = 2048, 2048, 1024
FLOPS = 2 * T * K * N

F32 = mybir.dt.float32
BF16 = mybir.dt.bfloat16
U32 = mybir.dt.uint32
U8 = mybir.dt.uint8
FP8 = mybir.dt.float8_e4m3fn
FP8X4 = mybir.dt.float8_e4m3fn_x4
MULT = mybir.AluOpType.mult
ADD = mybir.AluOpType.add
COPY = mybir.ActivationFunctionType.Copy
SIGMOID = mybir.ActivationFunctionType.Sigmoid

P = 128
PASSES = 4
X_TILES = T // P
W_TILES = N // P
HALF = 512

LOADS = [('w', 0, 1, 0), ('x', 0, 1, None), ('s', 0, 0, None), ('w', 0, 1, 1), ('b', 0, 0, None), ('w', 1, 1, None), ('w', 2, 1, None), ('x', 1, 1, None), ('w', 3, 1, None), ('x', 2, 1, None), ('w', 4, 1, None), ('w', 5, 1, None), ('w', 6, 1, None), ('x', 3, 1, None), ('w', 7, 1, None), ('x', 4, 2, None), ('x', 6, 2, None), ('x', 8, 2, None), ('x', 10, 2, None), ('x', 12, 2, None), ('x', 14, 2, None)]
ORDER = [
    ('D', 6), ('widen', 0), ('T', 'w', 0, 0), ('T', 'w', 0, 1), ('evac', 'w', 0, 0, 'S'), ('evac', 'w', 0, 1, 'V'),
    ('T', 'x', 0, 0), ('T', 'x', 0, 1), ('evac', 'x', 0, 0, 'S'), ('quant', 'w', 0), ('B',), ('evac', 'x', 0, 1, 'S'),
    ('T', 'w', 1, 0), ('Bc',), ('quant', 'x', 0), ('T', 'w', 1, 1), ('evac', 'w', 1, 0, 'S'), ('D', 1),
    ('widen', 1), ('T', 'w', 2, 0), ('evac', 'w', 1, 1, 'S'), ('T', 'w', 2, 1), ('evac', 'w', 2, 0, 'S'), ('quant', 'w', 1),
    ('D', 1), ('evac', 'w', 2, 1, 'S'), ('T', 'x', 1, 0), ('widen', 2), ('T', 'x', 1, 1), ('evac', 'x', 1, 0, 'S'),
    ('T', 'w', 3, 0), ('evac', 'x', 1, 1, 'S'), ('T', 'w', 3, 1), ('quant', 'w', 2), ('evac', 'w', 3, 0, 'S'), ('D', 1),
    ('T', 'x', 2, 0), ('quant', 'x', 1), ('evac', 'w', 3, 1, 'S'), ('T', 'x', 2, 1), ('T', 'w', 4, 0), ('evac', 'x', 2, 0, 'S'),
    ('quant', 'w', 3), ('T', 'w', 4, 1), ('evac', 'x', 2, 1, 'S'), ('M', 0, 0, 512), ('evac', 'w', 4, 0, 'S'), ('quant', 'x', 2),
    ('evac', 'w', 4, 1, 'S'), ('widen', 3), ('M', 1, 0, 512), ('add', 0, 0, 512), ('T', 'w', 5, 0), ('add', 1, 0, 512),
    ('sig', 0, 0, 512), ('T', 'w', 5, 1), ('widen', 4), ('evac', 'w', 5, 0, 'S'), ('T', 'w', 6, 0), ('evac', 'w', 5, 1, 'S'),
    ('T', 'w', 6, 1), ('quant', 'w', 4), ('M', 2, 0, 512), ('evac', 'w', 6, 0, 'S'), ('evac', 'w', 6, 1, 'S'), ('quant', 'w', 5),
    ('sig', 1, 0, 512), ('T', 'x', 3, 0), ('quant', 'w', 6), ('T', 'x', 3, 1), ('evac', 'x', 3, 0, 'S'), ('add', 2, 0, 512),
    ('T', 'w', 7, 0), ('evac', 'x', 3, 1, 'S'), ('widen', 5), ('T', 'w', 7, 1), ('evac', 'w', 7, 0, 'S'), ('T', 'x', 4, 0),
    ('T', 'x', 4, 1), ('evac', 'w', 7, 1, 'S'), ('quant', 'x', 3), ('sig', 2, 0, 512), ('quant', 'w', 7), ('M', 3, 0, 512),
    ('evac', 'x', 4, 0, 'S'), ('widen', 6), ('evac', 'x', 4, 1, 'S'), ('M', 0, 512, 512), ('add', 3, 0, 512), ('quant', 'x', 4),
    ('M', 1, 512, 512), ('sig', 3, 0, 512), ('add', 0, 512, 512), ('M', 2, 512, 512), ('add', 1, 512, 512), ('sig', 0, 512, 512),
    ('widen', 7), ('sig', 1, 512, 512), ('T', 'x', 5, 0), ('T', 'x', 5, 1), ('evac', 'x', 5, 0, 'S'), ('add', 2, 512, 512),
    ('T', 'x', 6, 0), ('T', 'x', 6, 1), ('evac', 'x', 5, 1, 'S'), ('widen', 8), ('M', 3, 512, 512), ('evac', 'x', 6, 0, 'S'),
    ('evac', 'x', 6, 1, 'S'), ('quant', 'x', 5), ('M', 4, 0, 512), ('sig', 2, 512, 512), ('add', 3, 512, 512), ('quant', 'x', 6),
    ('M', 4, 512, 512), ('sig', 3, 512, 512), ('add', 4, 0, 512), ('T', 'x', 7, 0), ('add', 4, 512, 512), ('sig', 4, 0, 512),
    ('T', 'x', 7, 1), ('widen', 9), ('evac', 'x', 7, 0, 'S'), ('T', 'x', 8, 0), ('T', 'x', 8, 1), ('evac', 'x', 7, 1, 'S'),
    ('M', 5, 0, 512), ('widen', 10), ('evac', 'x', 8, 0, 'S'), ('evac', 'x', 8, 1, 'S'), ('M', 5, 512, 512), ('sig', 4, 512, 512),
    ('add', 5, 0, 512), ('quant', 'x', 7), ('sig', 5, 0, 512), ('M', 6, 0, 512), ('add', 5, 512, 512), ('quant', 'x', 8),
    ('M', 6, 512, 512), ('sig', 5, 512, 512), ('add', 6, 0, 512), ('T', 'x', 9, 0), ('add', 6, 512, 512), ('sig', 6, 0, 512),
    ('T', 'x', 9, 1), ('widen', 11), ('evac', 'x', 9, 0, 'S'), ('T', 'x', 10, 0), ('T', 'x', 10, 1), ('evac', 'x', 9, 1, 'S'),
    ('M', 7, 0, 512), ('widen', 12), ('evac', 'x', 10, 0, 'S'), ('evac', 'x', 10, 1, 'S'), ('M', 7, 512, 512), ('sig', 6, 512, 512),
    ('add', 7, 0, 512), ('quant', 'x', 9), ('sig', 7, 0, 512), ('M', 8, 0, 512), ('add', 7, 512, 512), ('quant', 'x', 10),
    ('M', 8, 512, 512), ('sig', 7, 512, 512), ('add', 8, 0, 512), ('T', 'x', 11, 0), ('add', 8, 512, 512), ('sig', 8, 0, 512),
    ('T', 'x', 11, 1), ('widen', 13), ('evac', 'x', 11, 0, 'S'), ('T', 'x', 12, 0), ('T', 'x', 12, 1), ('evac', 'x', 11, 1, 'S'),
    ('M', 9, 0, 512), ('widen', 14), ('evac', 'x', 12, 0, 'S'), ('evac', 'x', 12, 1, 'S'), ('M', 9, 512, 512), ('sig', 8, 512, 512),
    ('add', 9, 0, 512), ('quant', 'x', 11), ('sig', 9, 0, 512), ('M', 10, 0, 512), ('add', 9, 512, 512), ('quant', 'x', 12),
    ('M', 10, 512, 512), ('sig', 9, 512, 512), ('add', 10, 0, 512), ('T', 'x', 13, 0), ('add', 10, 512, 512), ('sig', 10, 0, 512),
    ('T', 'x', 13, 1), ('widen', 15), ('evac', 'x', 13, 0, 'S'), ('T', 'x', 14, 0), ('T', 'x', 14, 1), ('evac', 'x', 13, 1, 'S'),
    ('M', 11, 0, 512), ('evac', 'x', 14, 0, 'S'), ('quant', 'x', 13), ('evac', 'x', 14, 1, 'S'), ('M', 11, 512, 512), ('add', 11, 0, 512),
    ('sig', 10, 512, 512), ('quant', 'x', 14), ('sig', 11, 0, 512), ('M', 12, 0, 512), ('add', 11, 512, 512), ('sig', 11, 512, 512),
    ('M', 12, 512, 512), ('add', 12, 0, 512), ('sig', 12, 0, 512), ('T', 'x', 15, 0), ('add', 12, 512, 512), ('T', 'x', 15, 1),
    ('evac', 'x', 15, 0, 'S'), ('M', 13, 0, 512), ('evac', 'x', 15, 1, 'S'), ('sig', 12, 512, 512), ('quant', 'x', 15), ('M', 13, 512, 512),
    ('add', 13, 0, 512), ('sig', 13, 0, 512), ('M', 14, 0, 512), ('add', 13, 512, 512), ('sig', 13, 512, 512), ('M', 14, 512, 512),
    ('add', 14, 0, 512), ('sig', 14, 0, 512), ('M', 15, 0, 512), ('add', 14, 512, 512), ('sig', 14, 512, 512), ('M', 15, 512, 256),
    ('add', 15, 0, 512), ('M', 15, 768, 256), ('add', 15, 512, 256), ('sig', 15, 0, 512), ('add', 15, 768, 256), ('sig', 15, 512, 256),
    ('sig', 15, 768, 256),
]


def tile_fp8_activation_linear_probe_d3_kernel(tc, x_bytes, x_scale, w, b, out):
    nc = tc.nc
    x_rows = x_bytes.rearrange("(p i) k -> p i k", i=X_TILES)
    out_rows = out.rearrange("(p i) n -> p i n", i=X_TILES)
    w_rows = w.rearrange("(j p) k -> p j k", p=P)

    with ExitStack() as ctx:
        keep = ctx.enter_context(tc.tile_pool(name="keep", bufs=1))
        wide_pool = ctx.enter_context(tc.tile_pool(name="wide", bufs=5))
        grouped_pool = ctx.enter_context(tc.tile_pool(name="grouped", bufs=5))
        result_pool = ctx.enter_context(tc.tile_pool(name="result", bufs=16))
        turn_psum = ctx.enter_context(tc.psum_pool(name="turn", bufs=4))
        acc_psum = ctx.enter_context(tc.psum_pool(name="acc", bufs=4))
        ctx.enter_context(tc.manual_schedule())

        xb = keep.tile([P, X_TILES, K], U8, name="xb", align_bytes=64)
        wb = keep.tile([P, W_TILES, K], BF16, name="wb", align_bytes=64)
        scale = keep.tile([P, X_TILES], F32, name="scale", align_bytes=64)
        x_codes = keep.tile([P, X_TILES, PASSES, P], U32, name="x_codes", align_bytes=64)
        x_scales = keep.tile([P, X_TILES, PASSES, P], U8, name="x_scales", align_bytes=64)
        w_codes = keep.tile([P, PASSES, N], U32, name="w_codes", align_bytes=64)
        w_scales = keep.tile([P, PASSES, N], U8, name="w_scales", align_bytes=64)
        ident = keep.tile([P, P], F32, name="ident", align_bytes=64)
        ones = keep.tile([P, P], BF16, name="ones", align_bytes=64)
        b_row = keep.tile([P, N], BF16, name="b_row", align_bytes=64)
        bias = keep.tile([P, N], BF16, name="bias", align_bytes=64)

        junk = keep.tile([P, HALF], BF16, name="junk", align_bytes=64)
        make_identity(nc, ident[:])
        nc.vector.memset(junk[:], 1.0)
        nc.vector.memset(b_row[:], 0.0)
        nc.vector.memset(ones[:], 64.0)
        nc.scalar.activation(out=ones[:], in_=ones[:], func=SIGMOID)

        for kind, first, count, part in LOADS:
            ks = slice(0, K) if part is None else slice(part * K // 2, (part + 1) * K // 2)
            if kind == "x":
                nc.sync.dma_start(out=xb[:, first : first + count, ks], in_=x_rows[:, first : first + count, ks])
            elif kind == "w":
                nc.sync.dma_start(out=wb[:, first : first + count, ks], in_=w_rows[:, first : first + count, ks])
            elif kind == "s":
                nc.sync.dma_start(out=scale[:], in_=x_scale.rearrange("(p i) o -> p (i o)", i=X_TILES))
            else:
                nc.sync.dma_start(out=b_row[0:1, :], in_=b.rearrange("(o n) -> o n", o=1))

        wide, plain, banks, grouped, accs, results = {}, {}, {}, {}, {}, {}

        def spread_bias():
            bank = acc_psum.tile([P, N], BF16, name="acc", tag="acc")
            banks["bias"] = bank
            for h in range(2):
                cols = slice(h * HALF, (h + 1) * HALF)
                nc.tensor.matmul(bank[:, cols], lhsT=ones[:], rhs=b_row[:, cols], start=True, stop=True)

        def copy_bias():
            nc.scalar.copy(out=bias[:], in_=banks["bias"][:])

        def warm(count):
            bank = acc_psum.tile([P, HALF], F32, name="acc", tag="acc")
            for r in range(count):
                nc.tensor.matmul(bank[:], lhsT=junk[:, 0:P], rhs=junk[:], start=True, stop=True)

        def scalar_widen(i):
            t = wide_pool.tile([P, K], BF16, name="wide", tag="wide", align_bytes=64)
            plain["x", i] = t
            nc.scalar.activation(out=t[:], in_=xb[:, i, :].bitcast(FP8), func=COPY, scale=scale[:, i : i + 1])

        def widen(i):
            t = wide_pool.tile([P, K], BF16, name="wide", tag="wide", align_bytes=64)
            wide["x", i] = t
            nc.vector.tensor_scalar(
                out=t[:].rearrange("p (u c e) -> p c u e", u=2, e=2),
                in0=xb[:, i, :].bitcast(FP8).rearrange("p (c u e) -> p c u e", u=2, e=2),
                scalar1=scale[:, i : i + 1],
                scalar2=None,
                op0=MULT,
            )

        def unzip(j, engine):
            t = wide_pool.tile([P, K], BF16, name="wide", tag="wide", align_bytes=64)
            wide["w", j] = t
            (nc.vector.tensor_copy if engine == "V" else nc.scalar.copy)(
                out=t[:].bitcast(F32).rearrange("p (u c) -> p u c", u=2),
                in_=wb[:, j, :].bitcast(F32).rearrange("p (c u) -> p u c", u=2),
            )

        def turn(kind, i, h):
            bank = turn_psum.tile([P, 2, 2, P], F32, name="turn", tag="turn")
            banks[kind, i, h] = bank
            for gg in range(2):
                g = 2 * h + gg
                for u in range(2):
                    if (kind, i) in wide:
                        src = wide[kind, i][:].bitcast(F32)[:, 512 * u + P * g : 512 * u + P * (g + 1)]
                    else:
                        rows = plain[kind, i][:] if kind == "x" else wb[:, i, :]
                        src = rows.bitcast(F32)[:, 256 * g + u : 256 * (g + 1) : 2]
                    nc.tensor.transpose(bank[:, gg, u, :], src, ident[:])

        def empty(kind, i, h, engine):
            if (kind, i) not in grouped:
                grouped[kind, i] = grouped_pool.tile([P, K], BF16, name="grouped", tag="grouped", align_bytes=64)
            dst = grouped[kind, i][:, 1024 * h : 1024 * (h + 1)].bitcast(F32).rearrange("p (g r u) -> p g r u", g=2, u=2)
            src = banks[kind, i, h][:].rearrange("p g u r -> p g r u")
            if engine == "S":
                nc.scalar.copy(out=dst, in_=src)
            else:
                nc.vector.tensor_copy(out=dst, in_=src)

        def quantise(kind, i):
            src = grouped[kind, i]
            if kind == "x":
                nc.vector.quantize_mx(
                    out=x_codes[:, i, :, :].rearrange("p g r -> p (g r)").bitcast(FP8X4),
                    scales=x_scales[:, i, :, :].rearrange("p g r -> p (g r)"),
                    in_=src[:],
                )
            else:
                for g in range(PASSES):
                    nc.vector.quantize_mx(
                        out=w_codes[:, g, P * i : P * (i + 1)].bitcast(FP8X4),
                        scales=w_scales[:, g, P * i : P * (i + 1)],
                        in_=src[:, 512 * g : 512 * (g + 1)],
                    )

        def multiply(i, c0, width):
            acc = acc_psum.tile([P, width], F32, name="acc", tag="acc")
            accs[i, c0] = acc
            cols = slice(c0, c0 + width)
            for g in range(PASSES):
                nc.tensor.matmul_mx(
                    out=acc[:],
                    lhsT=x_codes[:, i, g, :].bitcast(FP8X4),
                    lhsT_scale=x_scales[:, i, g, :],
                    rhs=w_codes[:, g, cols].bitcast(FP8X4),
                    rhs_scale=w_scales[:, g, cols],
                    start=(g == 0),
                    stop=(g == PASSES - 1),
                )

        def add_bias(i, c0, width):
            res = result_pool.tile([P, width], F32, name="res", tag="res", align_bytes=64)
            results[i, c0] = res
            nc.vector.tensor_tensor(out=res[:], in0=accs[i, c0][:], in1=bias[:, c0 : c0 + width], op=ADD)

        def finish(i, c0, width):
            res = results[i, c0]
            nc.scalar.activation(out=res[:], in_=res[:], func=SIGMOID)
            nc.sync.dma_start(out=out_rows[:, i, c0 : c0 + width], in_=res[:])

        steps = {"B": spread_bias, "Bc": copy_bias, "D": warm, "widen": widen, "swiden": scalar_widen, "unz": unzip, "T": turn,
                 "evac": empty, "quant": quantise, "M": multiply, "add": add_bias, "sig": finish}
        for step in ORDER:
            steps[step[0]](*step[1:])
